import numpy as np
import ml_dtypes


def mxq(x, axis, fmt="e4m3"):
    dtype, down = {"e4m3": (ml_dtypes.float8_e4m3fn, 7), "e5m2": (ml_dtypes.float8_e5m2, 14)}[fmt]
    v = np.moveaxis(np.asarray(x, np.float32).astype(ml_dtypes.bfloat16).astype(np.float64), axis, -1)
    blocks = v.reshape(v.shape[:-1] + (-1, 32))
    amax = np.abs(blocks).max(-1, keepdims=True)
    byte = np.maximum(np.where(amax > 0, np.frexp(amax)[1] - 1 + 127, 0) - down, 1)
    scale = np.exp2(byte - 127.0)
    codes = (blocks / scale).astype(np.float32).astype(dtype).astype(np.float64)
    return np.moveaxis((codes * scale).reshape(v.shape), -1, axis)


WIDE = False


def mx_kscale(k):
    if not WIDE:
        return np.ones(k)
    levels = np.array([30, -30])
    if k % 512:
        return np.exp2(np.random.permutation(np.resize(levels, k // 32))).repeat(32)
    a = np.empty((k // 512, 16))
    for p in range(k // 512):
        a[p, :8] = np.random.permutation(np.resize(levels, 8))
        for g in range(8):
            far = levels[np.abs(levels - a[p, g]) >= 10]
            a[p, g + 8] = far[np.random.randint(len(far))]
    return np.exp2(a.ravel()).repeat(32)


def f64(x):
    return np.asarray(x).astype(np.float64)


def striped(idx):
    return np.tile(np.asarray(idx).reshape(-1, 16).T, (8, 1)).astype(np.uint16)


def unstriped(offs):
    return offs[:16].T.reshape(-1).astype(np.int64)


E2M1 = np.array([0.0, 0.5, 1.0, 1.5, 2.0, 3.0, 4.0, 6.0, -0.0, -0.5, -1.0, -1.5, -2.0, -3.0, -4.0, -6.0])


def pack_weight(w, fmt):
    k, n = w.shape
    w = f64(np.asarray(w, np.float32).astype(ml_dtypes.bfloat16)).reshape(k // 32, 32, n)
    amax = np.abs(w).max(1)
    if fmt in ("e4m3", "e5m2"):
        byte = np.frexp(amax)[1] - 1 + 127 - (7 if fmt == "e4m3" else 14)
    else:
        mant, ex = np.frexp(amax / 6.0)
        byte = np.where(mant > 0.5, ex, ex - 1) + 127
    byte = np.clip(np.where(amax > 0, byte, 1), 1, 254)
    scaled = (w * np.exp2(127.0 - byte)[:, None, :]).reshape(k, n).astype(np.float32)
    by_word = np.ascontiguousarray(scaled.reshape(k // 512, 128, 4, n).transpose(0, 1, 3, 2))
    if fmt in ("e4m3", "e5m2"):
        words = by_word.astype(ml_dtypes.float8_e4m3fn if fmt == "e4m3" else ml_dtypes.float8_e5m2).view(np.uint8)
    else:
        c = by_word.astype(ml_dtypes.float4_e2m1fn).view(np.uint8) & 0xF
        words = (c[..., 0::2] | (c[..., 1::2] << 4)).reshape(k // 512, 128, 2 * n)
    return np.ascontiguousarray(words), np.ascontiguousarray(byte.astype(np.uint8).reshape(k // 512, 16, n))


def unpack_weight(words, scales, fmt):
    g, _, n = scales.shape
    words = np.ascontiguousarray(words).reshape(g, 128, n, -1)
    if fmt in ("e4m3", "e5m2"):
        vals = words.view(ml_dtypes.float8_e4m3fn if fmt == "e4m3" else ml_dtypes.float8_e5m2).astype(np.float64)
    else:
        nib = np.empty((g, 128, n, 4), np.uint8)
        nib[..., 0::2] = words & 0xF
        nib[..., 1::2] = words >> 4
        vals = E2M1[nib]
    vals = vals * np.repeat(np.exp2(scales.astype(np.float64) - 127.0), 8, axis=1)[..., None]
    return vals.transpose(0, 1, 3, 2).reshape(g * 512, n)


K, J, N, R, T, V, C = 512, 512, 256, 256, 1024, 1024, 64


def setup_inputs():
    n = np.random.standard_normal
    idx = np.random.permutation(T)[:J]
    idx2 = np.random.permutation(V)[:J]
    fj = mx_kscale(J)
    fk = mx_kscale(K)
    drp = pack_weight(n((K, R)) * 1 / np.sqrt(K) / fk[:, None], "e5m2")
    return {
        "xf": (n((K, T)) * np.random.uniform(0.4, 1.6, (1, T))).astype(np.float32),
        "ca": (np.random.uniform(0.5, 1.5, (J, 1)) * fj[:, None]).astype(np.float32),
        "gt": (n((N, V)) * np.exp(0.5 * n((1, V)))).astype(np.float32),
        "rb": (np.random.uniform(0.5, 1.5, (1, J)) / fj).astype(np.float32),
        "fkr": (np.random.uniform(0.5, 1.5, (1, K)) * fk).astype(np.float32),
        "dr_words": drp[0],
        "dr_scales": drp[1],
        "old": (1.0 * n((R, N))).astype(np.float32),
        "offs": striped(idx),
        "offs2": striped(idx2),
    }


def reference(xf, ca, gt, rb, fkr, dr_words, dr_scales, old, offs, offs2):
    idx = unstriped(offs)
    idx2 = unstriped(offs2)
    dru = unpack_weight(dr_words, dr_scales, "e5m2")
    xj = f64(xf)[:, idx].T
    uj = xj / (np.mean(np.abs(xj), axis=1, keepdims=True) + 0.1) * f64(ca) * f64(fkr)
    gg = f64(gt)[:, idx2]
    c1 = gg.reshape(N, C, J // C).mean(axis=2)
    c2 = np.repeat(c1, J // C, axis=1)
    gs = (gg - c2) * f64(rb)
    gj = gs.T
    ujq = mxq(uj, 0, "e4m3")
    gjq = mxq(gj, 0, "e5m2")
    w = ujq.T @ gjq
    wq = mxq(w, 0, "e5m2")
    v2 = dru.T @ wq
    y = 0.05 * v2 + 0.5 * f64(old)
    return y

@@ -1,0 +1,218 @@
+from contextlib import ExitStack
+
+import concourse.mybir as mybir
+from concourse.masks import make_identity
+
+K, J, N, R, T, V = 512, 512, 256, 256, 1024, 1024
+FLOPS = 2 * K * J * N + 2 * K * R * N
+
+F32 = mybir.dt.float32
+BF16 = mybir.dt.bfloat16
+U32 = mybir.dt.uint32
+I32 = mybir.dt.int32
+U16 = mybir.dt.uint16
+U8 = mybir.dt.uint8
+E4M3X4 = mybir.dt.float8_e4m3fn_x4
+E5M2X4 = mybir.dt.float8_e5m2_x4
+ALU = mybir.AluOpType
+ACT = mybir.ActivationFunctionType
+AX = mybir.AxisListType
+
+P = 128
+PACK = 4
+SET = 8
+G_SHARE = (256, 128)
+X_SHARE = (128, 192, 256, 256)
+
+
+def tile_list_directions_sized_centred_mixed_kernel(tc, xf, ca, gt, rb, fkr, dr_words, dr_scales, old, offs, offs2, out):
+    nc = tc.nc
+    halves = N // P
+
+    with ExitStack() as ctx:
+        sb = ctx.enter_context(tc.tile_pool(name="sb", bufs=1))
+        ps = ctx.enter_context(tc.psum_pool(name="ps", bufs=1))
+
+        x_list = sb.tile([P, J // 16], U16, name="x_list")
+        g_list = sb.tile([P, J // 16], U16, name="g_list")
+        g_win = [sb.tile([P, V], F32, name="g_win%d" % h) for h in range(halves)]
+        x_win = [sb.tile([P, T], F32, name="x_win%d" % t) for t in range(PACK)]
+        fkr_sb = sb.tile([P, PACK], F32, name="fkr_sb")
+        rb_sb = sb.tile([P, PACK], F32, name="rb_sb")
+        ca_sb = sb.tile([P, PACK], F32, name="ca_sb")
+        dr_codes = sb.tile([P, R], U32, name="dr_codes", align_bytes=64)
+        dr_plane = sb.tile([P, R], U8, name="dr_plane", align_bytes=64)
+        old_sb = sb.tile([P, R // P, N], F32, name="old_sb")
+        ident = sb.tile([P, P], F32, name="ident")
+
+        make_identity(nc, ident[:])
+        nc.vector.memset(dr_plane[:].bitcast(U32), 0)
+
+        xf_planes = xf.rearrange("(p t) c -> p t c", t=PACK)
+        nc.sync.dma_start(g_win[0][:], gt[0:P, :])
+        nc.sync.dma_start(g_list[:], offs2)
+        nc.sync.dma_start(g_win[1][:], gt[P : 2 * P, :])
+        nc.sync.dma_start(x_list[:], offs)
+        nc.sync.dma_start(fkr_sb[:], fkr.rearrange("o (p t) -> (o p) t", t=PACK))
+        nc.sync.dma_start(rb_sb[:], rb.rearrange("o (p t) -> (o p) t", t=PACK))
+        nc.sync.dma_start(ca_sb[:], ca.rearrange("(p t) o -> p (t o)", t=PACK))
+        for t in range(PACK):
+            nc.sync.dma_start(x_win[t][:], xf_planes[:, t, :])
+        nc.sync.dma_start(dr_codes[:].bitcast(I32), dr_words[0].rearrange("p c t -> p (c t)").bitcast(I32))
+        nc.sync.dma_start(old_sb[:], old.rearrange("(a p) n -> p a n", p=P))
+        for q in range(4):
+            nc.sync.dma_start(
+                dr_plane[32 * q : 32 * q + 4, :].bitcast(I32), dr_scales[0, 4 * q : 4 * q + 4, :].bitcast(I32)
+            )
+
+        def gather(dst, window, lst, n_vector):
+            if n_vector:
+                nc.vector.tensor_copy(dst[:, :n_vector], window[:].indirect(lst[:, : n_vector // 16]))
+            nc.scalar.activation(dst[:, n_vector:], window[:].indirect(lst[:, n_vector // 16 :]), ACT.Copy)
+
+        def dealt(tile_):
+            return tile_[:].rearrange("p t q -> p q t")
+
+        gg = [sb.tile([P, J], F32, name="gg%d" % h) for h in range(halves)]
+        xg_ring = [sb.tile([P, J], F32, name="xg%d" % i, tag="xg%d" % i, align_bytes=64) for i in range(2)]
+        set_sum = [xg_ring[h][:, : J // SET] for h in range(halves)]
+        g_bank = []
+        for h in range(halves):
+            gather(gg[h], g_win[h], g_list, G_SHARE[h])
+            nc.vector.tensor_reduce(set_sum[h], gg[h][:].rearrange("p (c e) -> p c e", e=SET), AX.X, ALU.add)
+            neg_mean = sb.tile([P, J // SET, 2], F32, name="neg_mean%d" % h)
+            nc.gpsimd.tensor_scalar(
+                neg_mean[:], set_sum[h].unsqueeze(2).to_broadcast([P, J // SET, 2]), -1.0 / SET, 0.0, ALU.mult, ALU.add
+            )
+            bank = ps.tile([P, PACK, P], F32, name="g_bank%d" % h, tag="gw%d" % h)
+            for t in range(PACK):
+                nc.tensor.matmul(
+                    bank[:, t, :], gg[h][:, t::PACK], ident[:], start=(t == 0), stop=False, is_transpose=True
+                )
+            for t in range(PACK):
+                nc.tensor.matmul(
+                    bank[:, t, :], neg_mean[:].rearrange("p c u -> p (c u)"), ident[:],
+                    start=False, stop=(t == PACK - 1), is_transpose=True,
+                )
+            g_bank.append(bank)
+
+        g_codes, g_plane = [], []
+
+        def quantise_gradients(h, gj):
+            nc.vector.tensor_tensor(
+                gj.rearrange("p (n t) -> p n t", t=PACK), dealt(g_bank[h]), rb_sb[:].unsqueeze(1).to_broadcast([P, P, PACK]), ALU.mult
+            )
+            codes = sb.tile([P, P], U32, name="g_codes%d" % h, align_bytes=64)
+            plane = sb.tile([P, P], U8, name="g_plane%d" % h, align_bytes=64)
+            nc.vector.quantize_mx(codes[:].bitcast(E5M2X4), plane[:], gj)
+            g_codes.append(codes)
+            g_plane.append(plane)
+
+        gj0 = sb.tile([P, J], BF16, name="gj0", align_bytes=64)
+        quantise_gradients(0, gj0[:])
+
+        abs_bank = [ps.tile([P, 2, P], F32, name="abs_bank%d" % i, tag="av%d" % i) for i in range(2)]
+        y_bank = []
+        for tk in range(PACK):
+            xg = xg_ring[tk % 2]
+            xg_v = xg[:].rearrange("p (q t) -> p q t", t=PACK)
+            gather(xg, x_win[tk], x_list, X_SHARE[tk])
+            mag = sb.tile([P, PACK, P], F32, name="mag%d" % tk)
+            scaled = sb.tile([P, PACK, P], F32, name="scaled%d" % tk)
+            if tk < PACK - 1:
+                nc.scalar.activation(dealt(mag), xg_v, ACT.Abs)
+            else:
+                nc.vector.scalar_tensor_tensor(
+                    dealt(mag)[:, :, :2], xg_v[:, :, :2], -1.0, xg_v[:, :, :2], ALU.mult, ALU.max
+                )
+                nc.scalar.activation(dealt(mag)[:, :, 2:], xg_v[:, :, 2:], ACT.Abs)
+            nc.vector.tensor_scalar(
+                dealt(scaled), xg_v, fkr_sb[:, tk : tk + 1], None, ALU.mult
+            )
+            for t in range(PACK):
+                nc.tensor.matmul(
+                    abs_bank[t // 2][:, t % 2, :],
+                    mag[:, t, :],
+                    ident[:],
+                    start=(tk == 0 and t % 2 == 0),
+                    stop=(tk == PACK - 1 and t % 2 == 1),
+                    is_transpose=True,
+                )
+            bank = ps.tile([P, PACK, P], F32, name="y_bank%d" % tk)
+            for t in range(PACK):
+                nc.tensor.transpose(bank[:, t, :], scaled[:, t, :], ident[:])
+            y_bank.append(bank)
+
+        gj1 = sb.tile([P, J], BF16, name="gj1", tag="xg1", align_bytes=64)
+        quantise_gradients(1, gj1[:])
+
+        den = sb.tile([P, PACK], F32, name="den")
+        terms_v = sb.tile([P, 2, P], BF16, name="terms_v")
+        terms_s = sb.tile([P, 2, P], BF16, name="terms_s", tag="scalar_late")
+        for i in range(2):
+            nc.vector.tensor_scalar(
+                terms_v[:, i, :], abs_bank[0][:, i, :], 1.0 / K, 0.1, ALU.mult, ALU.add, accum_out=den[:, i : i + 1]
+            )
+            nc.scalar.activation(
+                terms_s[:, i, :], abs_bank[1][:, i, :], ACT.Copy, bias=0.1 / P, scale=1.0 / K,
+                accum_out=den[:, 2 + i : 3 + i],
+            )
+        inv = sb.tile([P, PACK], F32, name="inv")
+        nc.vector.reciprocal(inv[:], den[:])
+        slot = sb.tile([P, PACK], F32, name="slot")
+        nc.vector.tensor_tensor(slot[:], inv[:], ca_sb[:], ALU.mult)
+
+        old_half = sb.tile([P, R // P, N], F32, name="old_half", tag="scalar_late")
+        nc.scalar.activation(old_half[:], old_sb[:], ACT.Copy, scale=0.5)
+
+        w_bank = [ps.tile([P, PACK, P], F32, name="w_bank%d" % h, tag="gw%d" % h) for h in range(halves)]
+        uj = []
+        for tk in range(PACK):
+            u = sb.tile([P, P, PACK], BF16, name="uj%d" % tk, align_bytes=64)
+            uj.append(u)
+
+        def scale_plane(tk):
+            if tk == PACK - 1:
+                for t in range(PACK):
+                    nc.scalar.activation(uj[tk][:, :, t], y_bank[tk][:, t, :], ACT.Copy, scale=slot[:, t : t + 1])
+                return
+            nc.vector.tensor_tensor(
+                uj[tk][:], dealt(y_bank[tk]), slot[:].unsqueeze(1).to_broadcast([P, P, PACK]), ALU.mult
+            )
+
+        def moment(tk):
+            codes = sb.tile([P, P], U32, name="u_codes%d" % tk, align_bytes=64)
+            plane = sb.tile([P, P], U8, name="u_plane%d" % tk, align_bytes=64)
+            nc.vector.quantize_mx(codes[:].bitcast(E4M3X4), plane[:], uj[tk][:].rearrange("p m t -> p (m t)"))
+            for h in range(halves):
+                nc.tensor.matmul_mx(
+                    w_bank[h][:, tk, :], lhsT=codes[:].bitcast(E4M3X4), lhsT_scale=plane[:],
+                    rhs=g_codes[h][:].bitcast(E5M2X4), rhs_scale=g_plane[h][:], start=True, stop=True,
+                )
+
+        scale_plane(0)
+        for tk in range(1, PACK):
+            scale_plane(tk)
+            moment(tk - 1)
+        moment(PACK - 1)
+
+        wb = [sb.tile([P, P, PACK], BF16, name="wb%d" % h, align_bytes=64) for h in range(halves)]
+        nc.scalar.copy(wb[0][:], dealt(w_bank[0]))
+        nc.vector.tensor_copy(wb[1][:], dealt(w_bank[1]))
+        out_v = out.rearrange("(a p) n -> p a n", p=P)
+        for h in range(halves):
+            codes = sb.tile([P, P], U32, name="w_codes%d" % h, align_bytes=64)
+            plane = sb.tile([P, P], U8, name="w_plane%d" % h, align_bytes=64)
+            nc.vector.quantize_mx(codes[:].bitcast(E5M2X4), plane[:], wb[h][:].rearrange("p n t -> p (n t)"))
+            v_bank = ps.tile([P, R // P, P], F32, name="v_bank%d" % h, tag="av%d" % h)
+            for a in range(R // P):
+                nc.tensor.matmul_mx(
+                    v_bank[:, a, :], lhsT=dr_codes[:, a * P : (a + 1) * P].bitcast(E5M2X4),
+                    lhsT_scale=dr_plane[:, a * P : (a + 1) * P],
+                    rhs=codes[:].bitcast(E5M2X4), rhs_scale=plane[:], start=True, stop=True,
+                )
+            y = sb.tile([P, R // P, P], F32, name="y%d" % h)
+            nc.vector.scalar_tensor_tensor(
+                y[:], v_bank[:], 0.05, old_half[:, :, h * P : (h + 1) * P], ALU.mult, ALU.add
+            )
+            nc.sync.dma_start(out_v[:, :, h * P : (h + 1) * P], y[:])

@@ -46,6 +46,9 @@ def tile_list_directions_sized_centred_mixed_kernel(tc, xf, ca, gt, rb, fkr, dr_
         ident = sb.tile([P, P], F32, name="ident")
 
         make_identity(nc, ident[:])
+        warm = sb.tile([P, 2], F32, name="warm")
+        nc.vector.memset(warm[:, 0:1], 0.0)
+        nc.scalar.activation(warm[:, 1:2], warm[:, 0:1], ACT.Abs)
         nc.vector.memset(dr_plane[:].bitcast(U32), 0)
 
         xf_planes = xf.rearrange("(p t) c -> p t c", t=PACK)

@@ -21,8 +21,8 @@ AX = mybir.AxisListType
 P = 128
 PACK = 4
 SET = 8
-G_SHARE = (256, 128)
-X_SHARE = (128, 192, 256, 256)
+G_SHARE = (256, 192)
+X_SHARE = (128, 512, 512, 512)
 
 
 def tile_list_directions_sized_centred_mixed_kernel(tc, xf, ca, gt, rb, fkr, dr_words, dr_scales, old, offs, offs2, out):
@@ -57,10 +57,10 @@ def tile_list_directions_sized_centred_mixed_kernel(tc, xf, ca, gt, rb, fkr, dr_
         nc.sync.dma_start(g_win[1][:], gt[P : 2 * P, :])
         nc.sync.dma_start(x_list[:], offs)
         nc.sync.dma_start(fkr_sb[:], fkr.rearrange("o (p t) -> (o p) t", t=PACK))
-        nc.sync.dma_start(rb_sb[:], rb.rearrange("o (p t) -> (o p) t", t=PACK))
-        nc.sync.dma_start(ca_sb[:], ca.rearrange("(p t) o -> p (t o)", t=PACK))
         for t in range(PACK):
             nc.sync.dma_start(x_win[t][:], xf_planes[:, t, :])
+        nc.sync.dma_start(rb_sb[:], rb.rearrange("o (p t) -> (o p) t", t=PACK))
+        nc.sync.dma_start(ca_sb[:], ca.rearrange("(p t) o -> p (t o)", t=PACK))
         nc.sync.dma_start(dr_codes[:].bitcast(I32), dr_words[0].rearrange("p c t -> p (c t)").bitcast(I32))
         nc.sync.dma_start(old_sb[:], old.rearrange("(a p) n -> p a n", p=P))
         for q in range(4):
@@ -71,14 +71,14 @@ def tile_list_directions_sized_centred_mixed_kernel(tc, xf, ca, gt, rb, fkr, dr_
         def gather(dst, window, lst, n_vector):
             if n_vector:
                 nc.vector.tensor_copy(dst[:, :n_vector], window[:].indirect(lst[:, : n_vector // 16]))
-            nc.scalar.activation(dst[:, n_vector:], window[:].indirect(lst[:, n_vector // 16 :]), ACT.Copy)
+            if n_vector < J:
+                nc.scalar.activation(dst[:, n_vector:], window[:].indirect(lst[:, n_vector // 16 :]), ACT.Copy)
 
         def dealt(tile_):
             return tile_[:].rearrange("p t q -> p q t")
 
         gg = [sb.tile([P, J], F32, name="gg%d" % h) for h in range(halves)]
-        xg_ring = [sb.tile([P, J], F32, name="xg%d" % i, tag="xg%d" % i, align_bytes=64) for i in range(2)]
-        set_sum = [xg_ring[h][:, : J // SET] for h in range(halves)]
+        set_sum = [sb.tile([P, J // SET], F32, name="set_sum%d" % h)[:] for h in range(halves)]
         g_bank = []
         for h in range(halves):
             gather(gg[h], g_win[h], g_list, G_SHARE[h])
@@ -111,13 +111,11 @@ def tile_list_directions_sized_centred_mixed_kernel(tc, xf, ca, gt, rb, fkr, dr_
             g_codes.append(codes)
             g_plane.append(plane)
 
-        gj0 = sb.tile([P, J], BF16, name="gj0", align_bytes=64)
-        quantise_gradients(0, gj0[:])
 
         abs_bank = [ps.tile([P, 2, P], F32, name="abs_bank%d" % i, tag="av%d" % i) for i in range(2)]
         y_bank = []
         for tk in range(PACK):
-            xg = xg_ring[tk % 2]
+            xg = sb.tile([P, J], F32, name="xg%d" % tk)
             xg_v = xg[:].rearrange("p (q t) -> p q t", t=PACK)
             gather(xg, x_win[tk], x_list, X_SHARE[tk])
             mag = sb.tile([P, PACK, P], F32, name="mag%d" % tk)
@@ -125,13 +123,9 @@ def tile_list_directions_sized_centred_mixed_kernel(tc, xf, ca, gt, rb, fkr, dr_
             if tk < PACK - 1:
                 nc.scalar.activation(dealt(mag), xg_v, ACT.Abs)
             else:
-                nc.vector.scalar_tensor_tensor(
-                    dealt(mag)[:, :, :2], xg_v[:, :, :2], -1.0, xg_v[:, :, :2], ALU.mult, ALU.max
-                )
+                nc.scalar.activation(dealt(mag)[:, :, :2], xg_v[:, :, :2], ACT.Abs)
                 nc.scalar.activation(dealt(mag)[:, :, 2:], xg_v[:, :, 2:], ACT.Abs)
-            nc.vector.tensor_scalar(
-                dealt(scaled), xg_v, fkr_sb[:, tk : tk + 1], None, ALU.mult
-            )
+            nc.scalar.activation(dealt(scaled), xg_v, ACT.Copy, scale=fkr_sb[:, tk : tk + 1])
             for t in range(PACK):
                 nc.tensor.matmul(
                     abs_bank[t // 2][:, t % 2, :],
@@ -146,8 +140,9 @@ def tile_list_directions_sized_centred_mixed_kernel(tc, xf, ca, gt, rb, fkr, dr_
                 nc.tensor.transpose(bank[:, t, :], scaled[:, t, :], ident[:])
             y_bank.append(bank)
 
-        gj1 = sb.tile([P, J], BF16, name="gj1", tag="xg1", align_bytes=64)
-        quantise_gradients(1, gj1[:])
+        for h in range(halves):
+            gj = sb.tile([P, J], BF16, name="gj%d" % h, align_bytes=64)
+            quantise_gradients(h, gj[:])
 
         den = sb.tile([P, PACK], F32, name="den")
         terms_v = sb.tile([P, 2, P], BF16, name="terms_v")
@@ -175,7 +170,7 @@ def tile_list_directions_sized_centred_mixed_kernel(tc, xf, ca, gt, rb, fkr, dr_
             uj.append(u)
 
         def scale_plane(tk):
-            if tk == PACK - 1:
+            if tk == 0:
                 for t in range(PACK):
                     nc.scalar.activation(uj[tk][:, :, t], y_bank[tk][:, t, :], ACT.Copy, scale=slot[:, t : t + 1])
                 return
@@ -194,10 +189,13 @@ def tile_list_directions_sized_centred_mixed_kernel(tc, xf, ca, gt, rb, fkr, dr_
                 )
 
         scale_plane(0)
-        for tk in range(1, PACK):
-            scale_plane(tk)
-            moment(tk - 1)
-        moment(PACK - 1)
+        scale_plane(1)
+        scale_plane(2)
+        moment(1)
+        scale_plane(3)
+        moment(2)
+        moment(0)
+        moment(3)
 
         wb = [sb.tile([P, P, PACK], BF16, name="wb%d" % h, align_bytes=64) for h in range(halves)]
         nc.scalar.copy(wb[0][:], dealt(w_bank[0]))

@@ -37,7 +37,7 @@ def tile_list_directions_sized_centred_mixed_kernel(tc, xf, ca, gt, rb, fkr, dr_
         g_list = sb.tile([P, J // 16], U16, name="g_list")
         g_win = [sb.tile([P, V], F32, name="g_win%d" % h) for h in range(halves)]
         x_win = [sb.tile([P, T], F32, name="x_win%d" % t) for t in range(PACK)]
-        fkr_sb = sb.tile([P, PACK], F32, name="fkr_sb")
+        fkr_sb = [sb.tile([P, 2], F32, name="fkr_sb%d" % i) for i in range(2)]
         rb_sb = sb.tile([P, PACK], F32, name="rb_sb")
         ca_sb = sb.tile([P, PACK], F32, name="ca_sb")
         dr_codes = sb.tile([P, R], U32, name="dr_codes", align_bytes=64)
@@ -56,10 +56,12 @@ def tile_list_directions_sized_centred_mixed_kernel(tc, xf, ca, gt, rb, fkr, dr_
         nc.sync.dma_start(g_list[:], offs2)
         nc.sync.dma_start(g_win[1][:], gt[P : 2 * P, :])
         nc.sync.dma_start(x_list[:], offs)
-        nc.sync.dma_start(fkr_sb[:], fkr.rearrange("o (p t) -> (o p) t", t=PACK))
+        fkr_v = fkr.rearrange("o (p t) -> (o p) t", t=PACK)
+        nc.sync.dma_start(fkr_sb[0][:], fkr_v[:, :2])
         for t in range(PACK):
             nc.sync.dma_start(x_win[t][:], xf_planes[:, t, :])
         nc.sync.dma_start(rb_sb[:], rb.rearrange("o (p t) -> (o p) t", t=PACK))
+        nc.sync.dma_start(fkr_sb[1][:], fkr_v[:, 2:])
         nc.sync.dma_start(ca_sb[:], ca.rearrange("(p t) o -> p (t o)", t=PACK))
         nc.sync.dma_start(dr_codes[:].bitcast(I32), dr_words[0].rearrange("p c t -> p (c t)").bitcast(I32))
         nc.sync.dma_start(old_sb[:], old.rearrange("(a p) n -> p a n", p=P))
@@ -81,7 +83,7 @@ def tile_list_directions_sized_centred_mixed_kernel(tc, xf, ca, gt, rb, fkr, dr_
         set_sum = [sb.tile([P, J // SET], F32, name="set_sum%d" % h)[:] for h in range(halves)]
         g_bank = []
         for h in range(halves):
-            gather(gg[h], g_win[h], g_list, G_SHARE[h])
+            gather(gg[h][:], g_win[h], g_list, G_SHARE[h])
             nc.vector.tensor_reduce(set_sum[h], gg[h][:].rearrange("p (c e) -> p c e", e=SET), AX.X, ALU.add)
             neg_mean = sb.tile([P, J // SET, 2], F32, name="neg_mean%d" % h)
             nc.gpsimd.tensor_scalar(
@@ -113,19 +115,18 @@ def tile_list_directions_sized_centred_mixed_kernel(tc, xf, ca, gt, rb, fkr, dr_
 
 
         abs_bank = [ps.tile([P, 2, P], F32, name="abs_bank%d" % i, tag="av%d" % i) for i in range(2)]
+        xg = [sb.tile([P, P, PACK], F32, name="xg%d" % tk) for tk in range(PACK)]
         y_bank = []
-        for tk in range(PACK):
-            xg = sb.tile([P, J], F32, name="xg%d" % tk)
-            xg_v = xg[:].rearrange("p (q t) -> p q t", t=PACK)
-            gather(xg, x_win[tk], x_list, X_SHARE[tk])
+
+        def magnitudes(tk):
+            gather(xg[tk][:].rearrange("p q t -> p (q t)"), x_win[tk], x_list, X_SHARE[tk])
             mag = sb.tile([P, PACK, P], F32, name="mag%d" % tk)
-            scaled = sb.tile([P, PACK, P], F32, name="scaled%d" % tk)
             if tk < PACK - 1:
-                nc.scalar.activation(dealt(mag), xg_v, ACT.Abs)
+                nc.scalar.activation(dealt(mag), xg[tk][:], ACT.Abs)
             else:
-                nc.scalar.activation(dealt(mag)[:, :, :2], xg_v[:, :, :2], ACT.Abs)
-                nc.scalar.activation(dealt(mag)[:, :, 2:], xg_v[:, :, 2:], ACT.Abs)
-            nc.scalar.activation(dealt(scaled), xg_v, ACT.Copy, scale=fkr_sb[:, tk : tk + 1])
+                for i in range(2):
+                    pair = slice(2 * i, 2 * i + 2)
+                    nc.scalar.activation(dealt(mag)[:, :, pair], xg[tk][:, :, pair], ACT.Abs)
             for t in range(PACK):
                 nc.tensor.matmul(
                     abs_bank[t // 2][:, t % 2, :],
@@ -135,25 +136,35 @@ def tile_list_directions_sized_centred_mixed_kernel(tc, xf, ca, gt, rb, fkr, dr_
                     stop=(tk == PACK - 1 and t % 2 == 1),
                     is_transpose=True,
                 )
+
+        def factored(tk):
+            scaled = sb.tile([P, PACK, P], F32, name="scaled%d" % tk)
+            factor = fkr_sb[tk // 2][:, tk % 2 : tk % 2 + 1]
+            if tk < 2:
+                nc.scalar.activation(dealt(scaled), xg[tk][:], ACT.Copy, scale=factor)
+            else:
+                nc.vector.tensor_scalar(dealt(scaled), xg[tk][:], factor, None, ALU.mult)
             bank = ps.tile([P, PACK, P], F32, name="y_bank%d" % tk)
             for t in range(PACK):
                 nc.tensor.transpose(bank[:, t, :], scaled[:, t, :], ident[:])
             y_bank.append(bank)
 
+        for tk in range(PACK):
+            magnitudes(tk)
+            if tk < 2:
+                factored(tk)
         for h in range(halves):
             gj = sb.tile([P, J], BF16, name="gj%d" % h, align_bytes=64)
             quantise_gradients(h, gj[:])
+        for tk in range(2, PACK):
+            factored(tk)
 
         den = sb.tile([P, PACK], F32, name="den")
-        terms_v = sb.tile([P, 2, P], BF16, name="terms_v")
-        terms_s = sb.tile([P, 2, P], BF16, name="terms_s", tag="scalar_late")
-        for i in range(2):
-            nc.vector.tensor_scalar(
-                terms_v[:, i, :], abs_bank[0][:, i, :], 1.0 / K, 0.1, ALU.mult, ALU.add, accum_out=den[:, i : i + 1]
-            )
+        terms = sb.tile([P, PACK, P], BF16, name="terms", tag="scalar_late")
+        for t in range(PACK):
             nc.scalar.activation(
-                terms_s[:, i, :], abs_bank[1][:, i, :], ACT.Copy, bias=0.1 / P, scale=1.0 / K,
-                accum_out=den[:, 2 + i : 3 + i],
+                terms[:, t, :], abs_bank[t // 2][:, t % 2, :], ACT.Copy, bias=0.1 / P, scale=1.0 / K,
+                accum_out=den[:, t : t + 1],
             )
         inv = sb.tile([P, PACK], F32, name="inv")
         nc.vector.reciprocal(inv[:], den[:])

@@ -21,210 +21,236 @@ AX = mybir.AxisListType
 P = 128
 PACK = 4
 SET = 8
-G_SHARE = (256, 192)
-X_SHARE = (128, 512, 512, 512)
+HALVES = N // P
+PER_COLUMN = 16
+PAIR = 2
+EARLY = 2
+
+G_ON_VECTOR = (256, 192)
+FIRST_QUARTER_ON_VECTOR = 128
 
 
-def tile_list_directions_sized_centred_mixed_kernel(tc, xf, ca, gt, rb, fkr, dr_words, dr_scales, old, offs, offs2, out):
+def tile_list_directions_sized_centred_mixed_kernel(
+    tc, xf, ca, gt, rb, fkr, dr_words, dr_scales, old, offs, offs2, out
+):
     nc = tc.nc
-    halves = N // P
 
     with ExitStack() as ctx:
         sb = ctx.enter_context(tc.tile_pool(name="sb", bufs=1))
         ps = ctx.enter_context(tc.psum_pool(name="ps", bufs=1))
 
-        x_list = sb.tile([P, J // 16], U16, name="x_list")
-        g_list = sb.tile([P, J // 16], U16, name="g_list")
-        g_win = [sb.tile([P, V], F32, name="g_win%d" % h) for h in range(halves)]
-        x_win = [sb.tile([P, T], F32, name="x_win%d" % t) for t in range(PACK)]
-        fkr_sb = [sb.tile([P, 2], F32, name="fkr_sb%d" % i) for i in range(2)]
+        x_list = sb.tile([P, J // PER_COLUMN], U16, name="x_list")
+        g_list = sb.tile([P, J // PER_COLUMN], U16, name="g_list")
+        g_win = [sb.tile([P, V], F32, name="g_win%d" % h) for h in range(HALVES)]
+        x_win = [sb.tile([P, T], F32, name="x_win%d" % a) for a in range(PACK)]
+        fkr_early = sb.tile([P, EARLY], F32, name="fkr_early")
+        fkr_late = sb.tile([P, PACK - EARLY], F32, name="fkr_late")
         rb_sb = sb.tile([P, PACK], F32, name="rb_sb")
         ca_sb = sb.tile([P, PACK], F32, name="ca_sb")
         dr_codes = sb.tile([P, R], U32, name="dr_codes", align_bytes=64)
-        dr_plane = sb.tile([P, R], U8, name="dr_plane", align_bytes=64)
+        dr_scale = sb.tile([P, R], U8, name="dr_scale", align_bytes=64)
         old_sb = sb.tile([P, R // P, N], F32, name="old_sb")
         ident = sb.tile([P, P], F32, name="ident")
 
         make_identity(nc, ident[:])
+
         warm = sb.tile([P, 2], F32, name="warm")
         nc.vector.memset(warm[:, 0:1], 0.0)
         nc.scalar.activation(warm[:, 1:2], warm[:, 0:1], ACT.Abs)
-        nc.vector.memset(dr_plane[:].bitcast(U32), 0)
 
-        xf_planes = xf.rearrange("(p t) c -> p t c", t=PACK)
+        nc.vector.memset(dr_scale[:].bitcast(U32), 0)
+
+        xf_quarters = xf.rearrange("(m a) c -> m a c", a=PACK)
+        fkr_quarters = fkr.rearrange("o (m a) -> (o m) a", a=PACK)
         nc.sync.dma_start(g_win[0][:], gt[0:P, :])
         nc.sync.dma_start(g_list[:], offs2)
         nc.sync.dma_start(g_win[1][:], gt[P : 2 * P, :])
         nc.sync.dma_start(x_list[:], offs)
-        fkr_v = fkr.rearrange("o (p t) -> (o p) t", t=PACK)
-        nc.sync.dma_start(fkr_sb[0][:], fkr_v[:, :2])
-        for t in range(PACK):
-            nc.sync.dma_start(x_win[t][:], xf_planes[:, t, :])
+        nc.sync.dma_start(fkr_early[:], fkr_quarters[:, :EARLY])
+        for a in range(PACK):
+            nc.sync.dma_start(x_win[a][:], xf_quarters[:, a, :])
         nc.sync.dma_start(rb_sb[:], rb.rearrange("o (p t) -> (o p) t", t=PACK))
-        nc.sync.dma_start(fkr_sb[1][:], fkr_v[:, 2:])
+        nc.sync.dma_start(fkr_late[:], fkr_quarters[:, EARLY:])
         nc.sync.dma_start(ca_sb[:], ca.rearrange("(p t) o -> p (t o)", t=PACK))
         nc.sync.dma_start(dr_codes[:].bitcast(I32), dr_words[0].rearrange("p c t -> p (c t)").bitcast(I32))
-        nc.sync.dma_start(old_sb[:], old.rearrange("(a p) n -> p a n", p=P))
-        for q in range(4):
+        nc.sync.dma_start(old_sb[:], old.rearrange("(i p) n -> p i n", p=P))
+        for q in range(P // 32):
             nc.sync.dma_start(
-                dr_plane[32 * q : 32 * q + 4, :].bitcast(I32), dr_scales[0, 4 * q : 4 * q + 4, :].bitcast(I32)
+                dr_scale[32 * q : 32 * q + 4, :].bitcast(I32), dr_scales[0, 4 * q : 4 * q + 4, :].bitcast(I32)
             )
 
-        def gather(dst, window, lst, n_vector):
-            if n_vector:
-                nc.vector.tensor_copy(dst[:, :n_vector], window[:].indirect(lst[:, : n_vector // 16]))
-            if n_vector < J:
-                nc.scalar.activation(dst[:, n_vector:], window[:].indirect(lst[:, n_vector // 16 :]), ACT.Copy)
+        def gather(dst, window, entries, on_vector):
+            cut = on_vector // PER_COLUMN
+            nc.vector.tensor_copy(dst[:, :on_vector], window[:].indirect(entries[:, :cut]))
+            if on_vector < J:
+                nc.scalar.activation(dst[:, on_vector:], window[:].indirect(entries[:, cut:]), ACT.Copy)
 
-        def dealt(tile_):
-            return tile_[:].rearrange("p t q -> p q t")
+        def inner_first(three_dims):
+            return three_dims[:].rearrange("p t c -> p c t")
 
-        gg = [sb.tile([P, J], F32, name="gg%d" % h) for h in range(halves)]
-        set_sum = [sb.tile([P, J // SET], F32, name="set_sum%d" % h)[:] for h in range(halves)]
-        g_bank = []
-        for h in range(halves):
-            gather(gg[h][:], g_win[h], g_list, G_SHARE[h])
-            nc.vector.tensor_reduce(set_sum[h], gg[h][:].rearrange("p (c e) -> p c e", e=SET), AX.X, ALU.add)
-            neg_mean = sb.tile([P, J // SET, 2], F32, name="neg_mean%d" % h)
+        gg = [sb.tile([P, J], F32, name="gg%d" % h) for h in range(HALVES)]
+        set_sum = [sb.tile([P, J // SET], F32, name="set_sum%d" % h) for h in range(HALVES)]
+        centred_bank = []
+        for h in range(HALVES):
+            gather(gg[h][:], g_win[h], g_list, G_ON_VECTOR[h])
+            nc.vector.tensor_reduce(set_sum[h][:], gg[h][:].rearrange("n (c e) -> n c e", e=SET), AX.X, ALU.add)
+            neg_mean = sb.tile([P, J // SET, SET // PACK], F32, name="neg_mean%d" % h)
             nc.gpsimd.tensor_scalar(
-                neg_mean[:], set_sum[h].unsqueeze(2).to_broadcast([P, J // SET, 2]), -1.0 / SET, 0.0, ALU.mult, ALU.add
+                neg_mean[:],
+                set_sum[h][:].unsqueeze(2).to_broadcast([P, J // SET, SET // PACK]),
+                -1.0 / SET,
+                0.0,
+                ALU.mult,
+                ALU.add,
             )
-            bank = ps.tile([P, PACK, P], F32, name="g_bank%d" % h, tag="gw%d" % h)
+            bank = ps.tile([P, PACK, P], F32, name="centred_bank%d" % h, tag="centred_then_w%d" % h)
             for t in range(PACK):
                 nc.tensor.matmul(
                     bank[:, t, :], gg[h][:, t::PACK], ident[:], start=(t == 0), stop=False, is_transpose=True
                 )
             for t in range(PACK):
                 nc.tensor.matmul(
-                    bank[:, t, :], neg_mean[:].rearrange("p c u -> p (c u)"), ident[:],
-                    start=False, stop=(t == PACK - 1), is_transpose=True,
+                    bank[:, t, :],
+                    neg_mean[:].rearrange("n c u -> n (c u)"),
+                    ident[:],
+                    start=False,
+                    stop=(t == PACK - 1),
+                    is_transpose=True,
                 )
-            g_bank.append(bank)
+            centred_bank.append(bank)
 
-        g_codes, g_plane = [], []
+        mag_bank = [
+            ps.tile([P, PAIR, P], F32, name="mag_bank%d" % i, tag="mag_then_v%d" % i) for i in range(PACK // PAIR)
+        ]
+        xg = [sb.tile([P, P, PACK], F32, name="xg%d" % a) for a in range(PACK)]
+        factored_bank = []
 
-        def quantise_gradients(h, gj):
-            nc.vector.tensor_tensor(
-                gj.rearrange("p (n t) -> p n t", t=PACK), dealt(g_bank[h]), rb_sb[:].unsqueeze(1).to_broadcast([P, P, PACK]), ALU.mult
-            )
-            codes = sb.tile([P, P], U32, name="g_codes%d" % h, align_bytes=64)
-            plane = sb.tile([P, P], U8, name="g_plane%d" % h, align_bytes=64)
-            nc.vector.quantize_mx(codes[:].bitcast(E5M2X4), plane[:], gj)
-            g_codes.append(codes)
-            g_plane.append(plane)
-
-
-        abs_bank = [ps.tile([P, 2, P], F32, name="abs_bank%d" % i, tag="av%d" % i) for i in range(2)]
-        xg = [sb.tile([P, P, PACK], F32, name="xg%d" % tk) for tk in range(PACK)]
-        y_bank = []
-
-        def magnitudes(tk):
-            gather(xg[tk][:].rearrange("p q t -> p (q t)"), x_win[tk], x_list, X_SHARE[tk])
-            mag = sb.tile([P, PACK, P], F32, name="mag%d" % tk)
-            if tk < PACK - 1:
-                nc.scalar.activation(dealt(mag), xg[tk][:], ACT.Abs)
+        def add_magnitudes(a):
+            on_vector = FIRST_QUARTER_ON_VECTOR if a == 0 else J
+            gather(xg[a][:].rearrange("m q t -> m (q t)"), x_win[a], x_list, on_vector)
+            mag = sb.tile([P, PACK, P], F32, name="mag%d" % a)
+            last = a == PACK - 1
+            if last:
+                for i in range(PACK // PAIR):
+                    pair = slice(PAIR * i, PAIR * (i + 1))
+                    nc.scalar.activation(inner_first(mag)[:, :, pair], xg[a][:, :, pair], ACT.Abs)
             else:
-                for i in range(2):
-                    pair = slice(2 * i, 2 * i + 2)
-                    nc.scalar.activation(dealt(mag)[:, :, pair], xg[tk][:, :, pair], ACT.Abs)
+                nc.scalar.activation(inner_first(mag), xg[a][:], ACT.Abs)
             for t in range(PACK):
                 nc.tensor.matmul(
-                    abs_bank[t // 2][:, t % 2, :],
+                    mag_bank[t // PAIR][:, t % PAIR, :],
                     mag[:, t, :],
                     ident[:],
-                    start=(tk == 0 and t % 2 == 0),
-                    stop=(tk == PACK - 1 and t % 2 == 1),
+                    start=(a == 0 and t % PAIR == 0),
+                    stop=(last and t % PAIR == PAIR - 1),
                     is_transpose=True,
                 )
 
-        def factored(tk):
-            scaled = sb.tile([P, PACK, P], F32, name="scaled%d" % tk)
-            factor = fkr_sb[tk // 2][:, tk % 2 : tk % 2 + 1]
-            if tk < 2:
-                nc.scalar.activation(dealt(scaled), xg[tk][:], ACT.Copy, scale=factor)
+        def apply_feature_factor(a):
+            factored = sb.tile([P, PACK, P], F32, name="factored%d" % a)
+            if a < EARLY:
+                nc.scalar.activation(inner_first(factored), xg[a][:], ACT.Copy, scale=fkr_early[:, a : a + 1])
             else:
-                nc.vector.tensor_scalar(dealt(scaled), xg[tk][:], factor, None, ALU.mult)
-            bank = ps.tile([P, PACK, P], F32, name="y_bank%d" % tk)
+                factor = fkr_late[:, a - EARLY : a - EARLY + 1]
+                nc.vector.tensor_scalar(inner_first(factored), xg[a][:], factor, None, ALU.mult)
+            bank = ps.tile([P, PACK, P], F32, name="factored_bank%d" % a)
             for t in range(PACK):
-                nc.tensor.transpose(bank[:, t, :], scaled[:, t, :], ident[:])
-            y_bank.append(bank)
+                nc.tensor.transpose(bank[:, t, :], factored[:, t, :], ident[:])
+            factored_bank.append(bank)
 
-        for tk in range(PACK):
-            magnitudes(tk)
-            if tk < 2:
-                factored(tk)
-        for h in range(halves):
-            gj = sb.tile([P, J], BF16, name="gj%d" % h, align_bytes=64)
-            quantise_gradients(h, gj[:])
-        for tk in range(2, PACK):
-            factored(tk)
+        for a in range(PACK):
+            add_magnitudes(a)
+            if a < EARLY:
+                apply_feature_factor(a)
+
+        g_codes, g_scale = [], []
+        for h in range(HALVES):
+            gj = sb.tile([P, P, PACK], BF16, name="gj%d" % h, align_bytes=64)
+            nc.vector.tensor_tensor(
+                gj[:], inner_first(centred_bank[h]), rb_sb[:].unsqueeze(1).to_broadcast([P, P, PACK]), ALU.mult
+            )
+            g_codes.append(sb.tile([P, P], U32, name="g_codes%d" % h, align_bytes=64))
+            g_scale.append(sb.tile([P, P], U8, name="g_scale%d" % h, align_bytes=64))
+            nc.vector.quantize_mx(g_codes[h][:].bitcast(E5M2X4), g_scale[h][:], gj[:].rearrange("p n t -> p (n t)"))
+
+        for a in range(EARLY, PACK):
+            apply_feature_factor(a)
 
         den = sb.tile([P, PACK], F32, name="den")
-        terms = sb.tile([P, PACK, P], BF16, name="terms", tag="scalar_late")
+        terms = sb.tile([P, PACK, P], F32, name="terms")
         for t in range(PACK):
             nc.scalar.activation(
-                terms[:, t, :], abs_bank[t // 2][:, t % 2, :], ACT.Copy, bias=0.1 / P, scale=1.0 / K,
+                terms[:, t, :],
+                mag_bank[t // PAIR][:, t % PAIR, :],
+                ACT.Copy,
+                bias=0.1 / P,
+                scale=1.0 / K,
                 accum_out=den[:, t : t + 1],
             )
-        inv = sb.tile([P, PACK], F32, name="inv")
-        nc.vector.reciprocal(inv[:], den[:])
-        slot = sb.tile([P, PACK], F32, name="slot")
-        nc.vector.tensor_tensor(slot[:], inv[:], ca_sb[:], ALU.mult)
+        inv_den = sb.tile([P, PACK], F32, name="inv_den")
+        nc.vector.reciprocal(inv_den[:], den[:])
+        slot_factor = sb.tile([P, PACK], F32, name="slot_factor", tag="slot_factor_then_old_half")
+        nc.vector.tensor_tensor(slot_factor[:], inv_den[:], ca_sb[:], ALU.mult)
 
-        old_half = sb.tile([P, R // P, N], F32, name="old_half", tag="scalar_late")
+        w_bank = [ps.tile([P, PACK, P], F32, name="w_bank%d" % h, tag="centred_then_w%d" % h) for h in range(HALVES)]
+        uj = [sb.tile([P, P, PACK], BF16, name="uj%d" % a, align_bytes=64) for a in range(PACK)]
+
+        def multiply(a):
+            codes = sb.tile([P, P], U32, name="u_codes%d" % a, align_bytes=64)
+            scale = sb.tile([P, P], U8, name="u_scale%d" % a, align_bytes=64)
+            nc.vector.quantize_mx(codes[:].bitcast(E4M3X4), scale[:], uj[a][:].rearrange("p m t -> p (m t)"))
+            for h in range(HALVES):
+                nc.tensor.matmul_mx(
+                    w_bank[h][:, a, :],
+                    lhsT=codes[:].bitcast(E4M3X4),
+                    lhsT_scale=scale[:],
+                    rhs=g_codes[h][:].bitcast(E5M2X4),
+                    rhs_scale=g_scale[h][:],
+                    start=True,
+                    stop=True,
+                )
+
+        for t in range(PACK):
+            nc.scalar.activation(uj[0][:, :, t], factored_bank[0][:, t, :], ACT.Copy, scale=slot_factor[:, t : t + 1])
+        for a in range(1, PACK):
+            nc.vector.tensor_tensor(
+                uj[a][:],
+                inner_first(factored_bank[a]),
+                slot_factor[:].unsqueeze(1).to_broadcast([P, P, PACK]),
+                ALU.mult,
+            )
+            if a > 1:
+                multiply(a - 1)
+        multiply(0)
+        multiply(PACK - 1)
+
+        old_half = sb.tile([P, R // P, N], F32, name="old_half", tag="slot_factor_then_old_half")
         nc.scalar.activation(old_half[:], old_sb[:], ACT.Copy, scale=0.5)
 
-        w_bank = [ps.tile([P, PACK, P], F32, name="w_bank%d" % h, tag="gw%d" % h) for h in range(halves)]
-        uj = []
-        for tk in range(PACK):
-            u = sb.tile([P, P, PACK], BF16, name="uj%d" % tk, align_bytes=64)
-            uj.append(u)
+        w_rounded = [sb.tile([P, P, PACK], BF16, name="w_rounded%d" % h, align_bytes=64) for h in range(HALVES)]
+        nc.scalar.copy(w_rounded[0][:], inner_first(w_bank[0]))
+        nc.vector.tensor_copy(w_rounded[1][:], inner_first(w_bank[1]))
 
-        def scale_plane(tk):
-            if tk == 0:
-                for t in range(PACK):
-                    nc.scalar.activation(uj[tk][:, :, t], y_bank[tk][:, t, :], ACT.Copy, scale=slot[:, t : t + 1])
-                return
-            nc.vector.tensor_tensor(
-                uj[tk][:], dealt(y_bank[tk]), slot[:].unsqueeze(1).to_broadcast([P, P, PACK]), ALU.mult
+        out_rows = out.rearrange("(i p) n -> p i n", p=P)
+        for h in range(HALVES):
+            columns = slice(h * P, (h + 1) * P)
+            w_codes = sb.tile([P, P], U32, name="w_codes%d" % h, align_bytes=64)
+            w_scale = sb.tile([P, P], U8, name="w_scale%d" % h, align_bytes=64)
+            nc.vector.quantize_mx(
+                w_codes[:].bitcast(E5M2X4), w_scale[:], w_rounded[h][:].rearrange("m c a -> m (c a)")
             )
-
-        def moment(tk):
-            codes = sb.tile([P, P], U32, name="u_codes%d" % tk, align_bytes=64)
-            plane = sb.tile([P, P], U8, name="u_plane%d" % tk, align_bytes=64)
-            nc.vector.quantize_mx(codes[:].bitcast(E4M3X4), plane[:], uj[tk][:].rearrange("p m t -> p (m t)"))
-            for h in range(halves):
+            v_bank = ps.tile([P, R // P, P], F32, name="v_bank%d" % h, tag="mag_then_v%d" % h)
+            for i in range(R // P):
+                directions = slice(i * P, (i + 1) * P)
                 nc.tensor.matmul_mx(
-                    w_bank[h][:, tk, :], lhsT=codes[:].bitcast(E4M3X4), lhsT_scale=plane[:],
-                    rhs=g_codes[h][:].bitcast(E5M2X4), rhs_scale=g_plane[h][:], start=True, stop=True,
-                )
-
-        scale_plane(0)
-        scale_plane(1)
-        scale_plane(2)
-        moment(1)
-        scale_plane(3)
-        moment(2)
-        moment(0)
-        moment(3)
-
-        wb = [sb.tile([P, P, PACK], BF16, name="wb%d" % h, align_bytes=64) for h in range(halves)]
-        nc.scalar.copy(wb[0][:], dealt(w_bank[0]))
-        nc.vector.tensor_copy(wb[1][:], dealt(w_bank[1]))
-        out_v = out.rearrange("(a p) n -> p a n", p=P)
-        for h in range(halves):
-            codes = sb.tile([P, P], U32, name="w_codes%d" % h, align_bytes=64)
-            plane = sb.tile([P, P], U8, name="w_plane%d" % h, align_bytes=64)
-            nc.vector.quantize_mx(codes[:].bitcast(E5M2X4), plane[:], wb[h][:].rearrange("p n t -> p (n t)"))
-            v_bank = ps.tile([P, R // P, P], F32, name="v_bank%d" % h, tag="av%d" % h)
-            for a in range(R // P):
-                nc.tensor.matmul_mx(
-                    v_bank[:, a, :], lhsT=dr_codes[:, a * P : (a + 1) * P].bitcast(E5M2X4),
-                    lhsT_scale=dr_plane[:, a * P : (a + 1) * P],
-                    rhs=codes[:].bitcast(E5M2X4), rhs_scale=plane[:], start=True, stop=True,
+                    v_bank[:, i, :],
+                    lhsT=dr_codes[:, directions].bitcast(E5M2X4),
+                    lhsT_scale=dr_scale[:, directions],
+                    rhs=w_codes[:].bitcast(E5M2X4),
+                    rhs_scale=w_scale[:],
+                    start=True,
+                    stop=True,
                 )
             y = sb.tile([P, R // P, P], F32, name="y%d" % h)
-            nc.vector.scalar_tensor_tensor(
-                y[:], v_bank[:], 0.05, old_half[:, :, h * P : (h + 1) * P], ALU.mult, ALU.add
-            )
-            nc.sync.dma_start(out_v[:, :, h * P : (h + 1) * P], y[:])
+            nc.vector.scalar_tensor_tensor(y[:], v_bank[:], 0.05, old_half[:, :, columns], ALU.mult, ALU.add)
+            nc.sync.dma_start(out_rows[:, :, columns], y[:])

from contextlib import ExitStack

import concourse.mybir as mybir
from concourse.masks import make_identity

K, J, N, R, T, V = 512, 512, 256, 256, 1024, 1024
FLOPS = 2 * K * J * N + 2 * K * R * N

F32 = mybir.dt.float32
BF16 = mybir.dt.bfloat16
U32 = mybir.dt.uint32
I32 = mybir.dt.int32
U16 = mybir.dt.uint16
U8 = mybir.dt.uint8
E4M3X4 = mybir.dt.float8_e4m3fn_x4
E5M2X4 = mybir.dt.float8_e5m2_x4
ALU = mybir.AluOpType
ACT = mybir.ActivationFunctionType
AX = mybir.AxisListType

P = 128
PACK = 4
SET = 8
HALVES = N // P
PER_COLUMN = 16
PAIR = 2
EARLY = 2

G_ON_VECTOR = (256, 192)
FIRST_QUARTER_ON_VECTOR = 128


def tile_list_directions_sized_centred_mixed_kernel(
    tc, xf, ca, gt, rb, fkr, dr_words, dr_scales, old, offs, offs2, out
):
    nc = tc.nc

    with ExitStack() as ctx:
        sb = ctx.enter_context(tc.tile_pool(name="sb", bufs=1))
        ps = ctx.enter_context(tc.psum_pool(name="ps", bufs=1))

        x_list = sb.tile([P, J // PER_COLUMN], U16, name="x_list")
        g_list = sb.tile([P, J // PER_COLUMN], U16, name="g_list")
        g_win = [sb.tile([P, V], F32, name="g_win%d" % h) for h in range(HALVES)]
        x_win = [sb.tile([P, T], F32, name="x_win%d" % a) for a in range(PACK)]
        fkr_early = sb.tile([P, EARLY], F32, name="fkr_early")
        fkr_late = sb.tile([P, PACK - EARLY], F32, name="fkr_late")
        rb_sb = sb.tile([P, PACK], F32, name="rb_sb")
        ca_sb = sb.tile([P, PACK], F32, name="ca_sb")
        dr_codes = sb.tile([P, R], U32, name="dr_codes", align_bytes=64)
        dr_scale = sb.tile([P, R], U8, name="dr_scale", align_bytes=64)
        old_sb = sb.tile([P, R // P, N], F32, name="old_sb")
        ident = sb.tile([P, P], F32, name="ident")

        make_identity(nc, ident[:])

        warm = sb.tile([P, 2], F32, name="warm")
        nc.vector.memset(warm[:, 0:1], 0.0)
        nc.scalar.activation(warm[:, 1:2], warm[:, 0:1], ACT.Abs)

        nc.vector.memset(dr_scale[:].bitcast(U32), 0)

        xf_quarters = xf.rearrange("(m a) c -> m a c", a=PACK)
        fkr_quarters = fkr.rearrange("o (m a) -> (o m) a", a=PACK)
        nc.sync.dma_start(g_win[0][:], gt[0:P, :])
        nc.sync.dma_start(g_list[:], offs2)
        nc.sync.dma_start(g_win[1][:], gt[P : 2 * P, :])
        nc.sync.dma_start(x_list[:], offs)
        nc.sync.dma_start(fkr_early[:], fkr_quarters[:, :EARLY])
        for a in range(PACK):
            nc.sync.dma_start(x_win[a][:], xf_quarters[:, a, :])
        nc.sync.dma_start(rb_sb[:], rb.rearrange("o (p t) -> (o p) t", t=PACK))
        nc.sync.dma_start(fkr_late[:], fkr_quarters[:, EARLY:])
        nc.sync.dma_start(ca_sb[:], ca.rearrange("(p t) o -> p (t o)", t=PACK))
        nc.sync.dma_start(dr_codes[:].bitcast(I32), dr_words[0].rearrange("p c t -> p (c t)").bitcast(I32))
        nc.sync.dma_start(old_sb[:], old.rearrange("(i p) n -> p i n", p=P))
        for q in range(P // 32):
            nc.sync.dma_start(
                dr_scale[32 * q : 32 * q + 4, :].bitcast(I32), dr_scales[0, 4 * q : 4 * q + 4, :].bitcast(I32)
            )

        def gather(dst, window, entries, on_vector):
            cut = on_vector // PER_COLUMN
            nc.vector.tensor_copy(dst[:, :on_vector], window[:].indirect(entries[:, :cut]))
            if on_vector < J:
                nc.scalar.activation(dst[:, on_vector:], window[:].indirect(entries[:, cut:]), ACT.Copy)

        def inner_first(three_dims):
            return three_dims[:].rearrange("p t c -> p c t")

        gg = [sb.tile([P, J], F32, name="gg%d" % h) for h in range(HALVES)]
        set_sum = [sb.tile([P, J // SET], F32, name="set_sum%d" % h) for h in range(HALVES)]
        centred_bank = []
        for h in range(HALVES):
            gather(gg[h][:], g_win[h], g_list, G_ON_VECTOR[h])
            nc.vector.tensor_reduce(set_sum[h][:], gg[h][:].rearrange("n (c e) -> n c e", e=SET), AX.X, ALU.add)
            neg_mean = sb.tile([P, J // SET, SET // PACK], F32, name="neg_mean%d" % h)
            nc.gpsimd.tensor_scalar(
                neg_mean[:],
                set_sum[h][:].unsqueeze(2).to_broadcast([P, J // SET, SET // PACK]),
                -1.0 / SET,
                0.0,
                ALU.mult,
                ALU.add,
            )
            bank = ps.tile([P, PACK, P], F32, name="centred_bank%d" % h, tag="centred_then_w%d" % h)
            for t in range(PACK):
                nc.tensor.matmul(
                    bank[:, t, :], gg[h][:, t::PACK], ident[:], start=(t == 0), stop=False, is_transpose=True
                )
            for t in range(PACK):
                nc.tensor.matmul(
                    bank[:, t, :],
                    neg_mean[:].rearrange("n c u -> n (c u)"),
                    ident[:],
                    start=False,
                    stop=(t == PACK - 1),
                    is_transpose=True,
                )
            centred_bank.append(bank)

        mag_bank = [
            ps.tile([P, PAIR, P], F32, name="mag_bank%d" % i, tag="mag_then_v%d" % i) for i in range(PACK // PAIR)
        ]
        xg = [sb.tile([P, P, PACK], F32, name="xg%d" % a) for a in range(PACK)]
        factored_bank = []

        def add_magnitudes(a):
            on_vector = FIRST_QUARTER_ON_VECTOR if a == 0 else J
            gather(xg[a][:].rearrange("m q t -> m (q t)"), x_win[a], x_list, on_vector)
            mag = sb.tile([P, PACK, P], F32, name="mag%d" % a)
            last = a == PACK - 1
            if last:
                for i in range(PACK // PAIR):
                    pair = slice(PAIR * i, PAIR * (i + 1))
                    nc.scalar.activation(inner_first(mag)[:, :, pair], xg[a][:, :, pair], ACT.Abs)
            else:
                nc.scalar.activation(inner_first(mag), xg[a][:], ACT.Abs)
            for t in range(PACK):
                nc.tensor.matmul(
                    mag_bank[t // PAIR][:, t % PAIR, :],
                    mag[:, t, :],
                    ident[:],
                    start=(a == 0 and t % PAIR == 0),
                    stop=(last and t % PAIR == PAIR - 1),
                    is_transpose=True,
                )

        def apply_feature_factor(a):
            factored = sb.tile([P, PACK, P], F32, name="factored%d" % a)
            if a < EARLY:
                nc.scalar.activation(inner_first(factored), xg[a][:], ACT.Copy, scale=fkr_early[:, a : a + 1])
            else:
                factor = fkr_late[:, a - EARLY : a - EARLY + 1]
                nc.vector.tensor_scalar(inner_first(factored), xg[a][:], factor, None, ALU.mult)
            bank = ps.tile([P, PACK, P], F32, name="factored_bank%d" % a)
            for t in range(PACK):
                nc.tensor.transpose(bank[:, t, :], factored[:, t, :], ident[:])
            factored_bank.append(bank)

        for a in range(PACK):
            add_magnitudes(a)
            if a < EARLY:
                apply_feature_factor(a)

        g_codes, g_scale = [], []
        for h in range(HALVES):
            gj = sb.tile([P, P, PACK], BF16, name="gj%d" % h, align_bytes=64)
            nc.vector.tensor_tensor(
                gj[:], inner_first(centred_bank[h]), rb_sb[:].unsqueeze(1).to_broadcast([P, P, PACK]), ALU.mult
            )
            g_codes.append(sb.tile([P, P], U32, name="g_codes%d" % h, align_bytes=64))
            g_scale.append(sb.tile([P, P], U8, name="g_scale%d" % h, align_bytes=64))
            nc.vector.quantize_mx(g_codes[h][:].bitcast(E5M2X4), g_scale[h][:], gj[:].rearrange("p n t -> p (n t)"))

        for a in range(EARLY, PACK):
            apply_feature_factor(a)

        den = sb.tile([P, PACK], F32, name="den")
        terms = sb.tile([P, PACK, P], F32, name="terms")
        for t in range(PACK):
            nc.scalar.activation(
                terms[:, t, :],
                mag_bank[t // PAIR][:, t % PAIR, :],
                ACT.Copy,
                bias=0.1 / P,
                scale=1.0 / K,
                accum_out=den[:, t : t + 1],
            )
        inv_den = sb.tile([P, PACK], F32, name="inv_den")
        nc.vector.reciprocal(inv_den[:], den[:])
        slot_factor = sb.tile([P, PACK], F32, name="slot_factor", tag="slot_factor_then_old_half")
        nc.vector.tensor_tensor(slot_factor[:], inv_den[:], ca_sb[:], ALU.mult)

        w_bank = [ps.tile([P, PACK, P], F32, name="w_bank%d" % h, tag="centred_then_w%d" % h) for h in range(HALVES)]
        uj = [sb.tile([P, P, PACK], BF16, name="uj%d" % a, align_bytes=64) for a in range(PACK)]

        def multiply(a):
            codes = sb.tile([P, P], U32, name="u_codes%d" % a, align_bytes=64)
            scale = sb.tile([P, P], U8, name="u_scale%d" % a, align_bytes=64)
            nc.vector.quantize_mx(codes[:].bitcast(E4M3X4), scale[:], uj[a][:].rearrange("p m t -> p (m t)"))
            for h in range(HALVES):
                nc.tensor.matmul_mx(
                    w_bank[h][:, a, :],
                    lhsT=codes[:].bitcast(E4M3X4),
                    lhsT_scale=scale[:],
                    rhs=g_codes[h][:].bitcast(E5M2X4),
                    rhs_scale=g_scale[h][:],
                    start=True,
                    stop=True,
                )

        for t in range(PACK):
            nc.scalar.activation(uj[0][:, :, t], factored_bank[0][:, t, :], ACT.Copy, scale=slot_factor[:, t : t + 1])
        for a in range(1, PACK):
            nc.vector.tensor_tensor(
                uj[a][:],
                inner_first(factored_bank[a]),
                slot_factor[:].unsqueeze(1).to_broadcast([P, P, PACK]),
                ALU.mult,
            )
            if a > 1:
                multiply(a - 1)
        multiply(0)
        multiply(PACK - 1)

        old_half = sb.tile([P, R // P, N], F32, name="old_half", tag="slot_factor_then_old_half")
        nc.scalar.activation(old_half[:], old_sb[:], ACT.Copy, scale=0.5)

        w_rounded = [sb.tile([P, P, PACK], BF16, name="w_rounded%d" % h, align_bytes=64) for h in range(HALVES)]
        nc.scalar.copy(w_rounded[0][:], inner_first(w_bank[0]))
        nc.vector.tensor_copy(w_rounded[1][:], inner_first(w_bank[1]))

        out_rows = out.rearrange("(i p) n -> p i n", p=P)
        for h in range(HALVES):
            columns = slice(h * P, (h + 1) * P)
            w_codes = sb.tile([P, P], U32, name="w_codes%d" % h, align_bytes=64)
            w_scale = sb.tile([P, P], U8, name="w_scale%d" % h, align_bytes=64)
            nc.vector.quantize_mx(
                w_codes[:].bitcast(E5M2X4), w_scale[:], w_rounded[h][:].rearrange("m c a -> m (c a)")
            )
            v_bank = ps.tile([P, R // P, P], F32, name="v_bank%d" % h, tag="mag_then_v%d" % h)
            for i in range(R // P):
                directions = slice(i * P, (i + 1) * P)
                nc.tensor.matmul_mx(
                    v_bank[:, i, :],
                    lhsT=dr_codes[:, directions].bitcast(E5M2X4),
                    lhsT_scale=dr_scale[:, directions],
                    rhs=w_codes[:].bitcast(E5M2X4),
                    rhs_scale=w_scale[:],
                    start=True,
                    stop=True,
                )
            y = sb.tile([P, R // P, P], F32, name="y%d" % h)
            nc.vector.scalar_tensor_tensor(y[:], v_bank[:], 0.05, old_half[:, :, columns], ALU.mult, ALU.add)
            nc.sync.dma_start(out_rows[:, :, columns], y[:])
